import numpy as np
import ml_dtypes


def mxq(x, axis, fmt="e4m3"):
    dtype, down = {"e4m3": (ml_dtypes.float8_e4m3fn, 7), "e5m2": (ml_dtypes.float8_e5m2, 14)}[fmt]
    v = np.moveaxis(np.asarray(x, np.float32).astype(ml_dtypes.bfloat16).astype(np.float64), axis, -1)
    blocks = v.reshape(v.shape[:-1] + (-1, 32))
    amax = np.abs(blocks).max(-1, keepdims=True)
    byte = np.maximum(np.where(amax > 0, np.frexp(amax)[1] - 1 + 127, 0) - down, 1)
    scale = np.exp2(byte - 127.0)
    codes = (blocks / scale).astype(np.float32).astype(dtype).astype(np.float64)
    return np.moveaxis((codes * scale).reshape(v.shape), -1, axis)


WIDE = False


def mx_kscale(k):
    if not WIDE:
        return np.ones(k)
    levels = np.array([10, -10, 5, -5, 0])
    if k % 512:
        return np.exp2(np.random.permutation(np.resize(levels, k // 32))).repeat(32)
    a = np.empty((k // 512, 16))
    for p in range(k // 512):
        a[p, :8] = np.random.permutation(np.resize(levels, 8))
        for g in range(8):
            far = levels[np.abs(levels - a[p, g]) >= 10]
            a[p, g + 8] = far[np.random.randint(len(far))]
    return np.exp2(a.ravel()).repeat(32)


def f64(x):
    return np.asarray(x).astype(np.float64)


def striped(idx):
    return np.tile(idx.reshape(-1, 16).T, (8, 1)).astype(np.uint16)


def unstriped(offs):
    return offs[:16].T.reshape(-1).astype(np.int64)


E2M1 = np.array([0.0, 0.5, 1.0, 1.5, 2.0, 3.0, 4.0, 6.0, -0.0, -0.5, -1.0, -1.5, -2.0, -3.0, -4.0, -6.0])


def pack_weight(w, fmt):
    k, n = w.shape
    w = f64(np.asarray(w, np.float32).astype(ml_dtypes.bfloat16)).reshape(k // 32, 32, n)
    amax = np.abs(w).max(1)
    if fmt == "e4m3":
        byte = np.frexp(amax)[1] - 1 + 127 - 7
    else:
        mant, ex = np.frexp(amax / 6.0)
        byte = np.where(mant > 0.5, ex, ex - 1) + 127
    byte = np.clip(np.where(amax > 0, byte, 1), 1, 254)
    scaled = (w * np.exp2(127.0 - byte)[:, None, :]).reshape(k, n).astype(np.float32)
    by_word = np.ascontiguousarray(scaled.reshape(k // 512, 128, 4, n).transpose(0, 1, 3, 2))
    if fmt == "e4m3":
        words = by_word.astype(ml_dtypes.float8_e4m3fn).view(np.uint8)
    else:
        c = by_word.astype(ml_dtypes.float4_e2m1fn).view(np.uint8) & 0xF
        words = (c[..., 0::2] | (c[..., 1::2] << 4)).reshape(k // 512, 128, 2 * n)
    return np.ascontiguousarray(words), np.ascontiguousarray(byte.astype(np.uint8).reshape(k // 512, 16, n))


def unpack_weight(words, scales, fmt):
    g, _, n = scales.shape
    words = np.ascontiguousarray(words).reshape(g, 128, n, -1)
    if fmt == "e4m3":
        vals = words.view(ml_dtypes.float8_e4m3fn).astype(np.float64)
    else:
        nib = np.empty((g, 128, n, 4), np.uint8)
        nib[..., 0::2] = words & 0xF
        nib[..., 1::2] = words >> 4
        vals = E2M1[nib]
    vals = vals * np.repeat(np.exp2(scales.astype(np.float64) - 127.0), 8, axis=1)[..., None]
    return vals.transpose(0, 1, 3, 2).reshape(g * 512, n)


def gelu(v):
    return 0.5 * v * (1.0 + np.tanh(np.sqrt(2.0 / np.pi) * (v + 0.044715 * v**3)))


def bf(x):
    return np.asarray(x, np.float32).astype(ml_dtypes.bfloat16)


def planes(Y):
    n, m = Y.shape
    b = f64(bf(Y)).reshape(n // 32, 32, m)
    amax = np.abs(b).max(1)
    byte = np.clip(np.where(amax > 0, np.frexp(amax)[1] - 1 + 127 - 7, 1), 1, 254)
    codes = (b * np.exp2(127.0 - byte)[:, None, :]).reshape(n, m).astype(np.float32).astype(ml_dtypes.float8_e4m3fn).view(np.uint8)
    words = codes.reshape(n // 512, 128, 4, m).transpose(0, 1, 3, 2)
    return np.ascontiguousarray(words), np.ascontiguousarray(byte.astype(np.uint8).reshape(n // 512, 16, m))


K, H, N, T, S, P = 1024, 1024, 512, 2048, 1024, 512

def setup_inputs():
    n = np.random.standard_normal
    s = mx_kscale(K)[:, None]
    u = mx_kscale(H)[:, None]
    tab_words, tab_scales = pack_weight(n((K, T)) * s, "e4m3")
    w1 = (n((K, H)) / np.sqrt(K) / s * u.T).astype(np.float32)
    floor = ((-0.7 + 0.4 * n(H)) * u[:, 0]).astype(np.float32)
    wa_words, wa_scales = pack_weight(1.2 * n((H, N)) / np.sqrt(H) / u, "e2m1")
    wb = (n((K, N)) / np.sqrt(K) / s).astype(np.float32)
    temp = np.random.uniform(0.4, 1.6, N).astype(np.float32)
    shift = (0.5 * n(N)).astype(np.float32)
    base = (n((N, P)) * np.exp(0.8 * n(N))[:, None]).astype(np.float32)
    return {"tab_words": tab_words, "tab_scales": tab_scales,
            "offs": striped(np.random.permutation(T)[:S]),
            "pos1": striped(np.random.permutation(S)[:P]),
            "pos2": striped(np.random.permutation(S)[:P]),
            "w1": w1, "floor": floor, "wa_words": wa_words, "wa_scales": wa_scales,
            "wb": wb, "temp": temp, "shift": shift, "base": base}

def reference(tab_words, tab_scales, offs, pos1, pos2, w1, floor, wa_words, wa_scales, wb, temp, shift, base):
    v = unpack_weight(tab_words, tab_scales, "e4m3")[:, unstriped(offs)]
    h = np.maximum(mxq(f64(w1), 0, "e4m3").T @ v, f64(floor)[:, None])
    hq = mxq(h, 0, "e4m3")
    ah = unpack_weight(wa_words, wa_scales, "e2m1").T @ hq
    bv = mxq(f64(wb), 0, "e4m3").T @ v
    e = np.minimum(np.maximum(ah * bv, -2.0), 2.0)
    a = np.exp(f64(temp)[:, None] * e[:, unstriped(pos1)] + f64(shift)[:, None])
    c = e[:, unstriped(pos2)]
    y = (a - f64(base)) * np.sin(c)
    words, scales = planes(y)
    return y, words, scales

@@ -1,0 +1,309 @@
+from contextlib import ExitStack
+
+import concourse.mybir as mybir
+
+K, H, N, T, S, M = 1024, 1024, 512, 2048, 1024, 512
+FLOPS = 2 * S * (K * H + H * N + K * N)
+
+F32 = mybir.dt.float32
+BF16 = mybir.dt.bfloat16
+I32 = mybir.dt.int32
+U32 = mybir.dt.uint32
+U16 = mybir.dt.uint16
+U8 = mybir.dt.uint8
+FP8X4 = mybir.dt.float8_e4m3fn_x4
+FP4X4 = mybir.dt.float4_e2m1fn_x4
+ALU = mybir.AluOpType
+ACT = mybir.ActivationFunctionType
+
+P = 128
+PACK = 4
+KP = P * PACK
+HALF = 512
+NB = 128
+
+
+def tile_list_burst_band_features_kernel(
+    tc, tab_words, tab_scales, offs, pos1, pos2, w1, floor, wa_words, wa_scales, wb, temp, shift, base,
+    out_0, out_1, out_2,
+):
+    nc = tc.nc
+    with ExitStack() as ctx:
+        keep = ctx.enter_context(tc.tile_pool(name="keep", bufs=1))
+        ring = ctx.enter_context(tc.tile_pool(name="ring", bufs=3))
+        psum = ctx.enter_context(tc.psum_pool(name="psum", bufs=8))
+
+        def sb(name, shape, dtype, tag=None):
+            return keep.tile(shape, dtype, name=name, tag=tag or name, align_bytes=64)
+
+        offs_sb = keep.tile([P, S // 16], U16, name="offs_sb")
+        pos1_sb = keep.tile([P, M // 16], U16, name="pos1_sb")
+        pos2_sb = keep.tile([P, M // 16], U16, name="pos2_sb")
+
+        tab_w = [sb("tab_w%d" % a, [P, T], U32) for a in range(2)]
+        tab_s = sb("tab_s", [P, T], U8)
+        tab_s_rows = sb("tab_s_rows", [P, T // 4], I32)
+        wa_w = sb("wa_w", [P, 2, 2 * N], U8)
+        wa_s = sb("wa_s", [P, 2, N], U8)
+        floor_sb = sb("floor_sb", [P, 2, PACK], F32)
+        temp_sb = sb("temp_sb", [P, PACK], F32)
+        shift_sb = sb("shift_sb", [P, PACK], F32)
+        base_sb = sb("base_sb", [P, PACK, M], F32)
+
+        nc.vector.memset(tab_s[:].bitcast(I32), 0)
+        nc.gpsimd.memset(wa_s[:].rearrange("p a n -> p (a n)").bitcast(I32), 0)
+
+        raw = {}
+        weight_rows = {"w%d%d" % (b, a): w1[a * KP:(a + 1) * KP, b * KP:(b + 1) * KP] for b in range(2) for a in range(2)}
+        weight_rows.update({"wb%d" % a: wb[a * KP:(a + 1) * KP, :] for a in range(2)})
+
+        def load_weight(name):
+            raw[name] = sb("raw_" + name, [P, PACK, KP], F32)
+            nc.sync.dma_start(out=raw[name][:], in_=weight_rows[name].rearrange("(p j) c -> p j c", j=PACK))
+
+        def load_tab(a):
+            nc.sync.dma_start(out=tab_w[a][:].bitcast(I32), in_=tab_words[a].rearrange("p t i -> p (t i)").bitcast(I32))
+
+        def load_tab_scales():
+            for q in range(4):
+                nc.sync.dma_start(out=tab_s_rows[32 * q:32 * q + 8, :], in_=tab_scales[:, 4 * q:4 * q + 4, :].bitcast(I32))
+
+        def load_wa():
+            nc.sync.dma_start(out=wa_w[:].bitcast(I32), in_=wa_words.rearrange("a p c -> p a c").bitcast(I32))
+            for q in range(4):
+                nc.sync.dma_start(out=wa_s[32 * q:32 * q + 4, :, :].bitcast(I32),
+                                  in_=wa_scales[:, 4 * q:4 * q + 4, :].rearrange("a r n -> r a n").bitcast(I32))
+
+        def load_small(tile, vec):
+            nc.sync.dma_start(out=tile[:], in_=vec)
+
+        nc.sync.dma_start(offs_sb[:], offs)
+        load_small(floor_sb, floor.rearrange("(b p t) -> p b t", b=2, t=PACK))
+        load_tab_scales()
+        load_weight("w00")
+        load_tab(0)
+        load_weight("w01")
+        load_tab(1)
+        load_weight("w10")
+        load_weight("w11")
+        load_wa()
+        load_weight("wb0")
+        load_weight("wb1")
+        nc.sync.dma_start(pos1_sb[:], pos1)
+        nc.sync.dma_start(pos2_sb[:], pos2)
+        load_small(temp_sb, temp.rearrange("(p t) -> p t", t=PACK))
+        load_small(shift_sb, shift.rearrange("(p t) -> p t", t=PACK))
+        load_small(base_sb, base.rearrange("(p t) m -> p t m", t=PACK))
+
+        for q in range(4):
+            nc.vector.tensor_copy(out=tab_s[32 * q:32 * q + 8, :].bitcast(I32), in_=tab_s_rows[32 * q:32 * q + 8, :])
+        floor_bf = sb("floor_bf", [P, 2, 16, PACK], BF16)
+        nc.vector.tensor_copy(out=floor_bf[:], in_=floor_sb[:].unsqueeze(2).to_broadcast([P, 2, 16, PACK]))
+
+        codes = {}
+        scales = {}
+        grouped = {}
+
+        def cast_weight(name, on_vector, on_gpsimd):
+            grouped[name] = ring.tile([P, PACK, P, PACK], BF16, name="grouped", align_bytes=64)
+            dst = grouped[name][:].rearrange("p t m j -> p m j t")
+            src = raw[name][:].rearrange("p j (m t) -> p m j t", t=PACK)
+            if on_vector > 0:
+                nc.vector.tensor_copy(out=dst[:, 0:on_vector], in_=src[:, 0:on_vector])
+            for m0 in range(on_vector, on_vector + on_gpsimd, 32):
+                nc.gpsimd.tensor_scalar(out=dst[:, m0:m0 + 32], in0=src[:, m0:m0 + 32], scalar1=1.0, scalar2=0.0,
+                                        op0=ALU.mult, op1=ALU.add)
+            if on_vector + on_gpsimd < P:
+                nc.scalar.copy(out=dst[:, on_vector + on_gpsimd:P], in_=src[:, on_vector + on_gpsimd:P])
+
+        def quantise_weight(name):
+            codes[name] = sb("codes_" + name, [P, KP], U32)
+            scales[name] = sb("scales_" + name, [P, KP], U8)
+            nc.vector.quantize_mx(out=codes[name][:].bitcast(FP8X4), scales=scales[name][:],
+                                  in_=grouped[name][:].rearrange("p t m j -> p (t m j)"))
+
+        v_w = {}
+        v_s = {}
+
+        def gather_scales(hf):
+            v_s[hf] = sb("v_s%d" % hf, [P, HALF], U8)
+            nc.vector.tensor_copy(out=v_s[hf][:], in_=tab_s[:].indirect(offs_sb[:, 32 * hf:32 * hf + 32]))
+
+        def gather_words(a, hf):
+            v_w[a, hf] = sb("v_w%d%d" % (a, hf), [P, HALF], U32)
+            nc.vector.tensor_copy(out=v_w[a, hf][:], in_=tab_w[a][:].indirect(offs_sb[:, 32 * hf:32 * hf + 32]))
+
+        h_banks = {}
+        h_grp = {}
+        h_codes = {}
+        h_scales = {}
+
+        def h_passes(b, a, hf):
+            name = "w%d%d" % (b, a)
+            for i in range(HALF // NB):
+                if a == 0:
+                    h_banks[b, hf, i] = psum.tile([P, PACK, NB], F32, name="bank")
+                c0 = i * NB
+                for t in range(PACK):
+                    nc.tensor.matmul_mx(
+                        out=h_banks[b, hf, i][:, t, :],
+                        lhsT=codes[name][:, t * P:(t + 1) * P].bitcast(FP8X4),
+                        lhsT_scale=scales[name][:, t * P:(t + 1) * P],
+                        rhs=v_w[a, hf][:, c0:c0 + NB].bitcast(FP8X4),
+                        rhs_scale=v_s[hf][4 * a:P, c0:c0 + NB],
+                        start=(a == 0 and t == 0), stop=(a == 1 and t == PACK - 1),
+                    )
+
+        def h_exit(b, hf, how):
+            h_grp[b, hf] = sb("h_grp%d%d" % (b, hf), [P, HALF, PACK], BF16)
+            on_scalar = []
+            for i in range(HALF // NB):
+                cols = h_grp[b, hf][:, i * NB:(i + 1) * NB, :]
+                sums = h_banks[b, hf, i][:].rearrange("p t n -> p n t")
+                if how[i] == "V":
+                    nc.vector.tensor_tensor(out=cols, in0=sums, in1=floor_sb[:, b:b + 1, :].to_broadcast([P, NB, PACK]), op=ALU.max)
+                else:
+                    nc.scalar.copy(out=cols, in_=sums)
+                    on_scalar.append(i)
+            if on_scalar:
+                lo, hi = on_scalar[0] * NB, (on_scalar[-1] + 1) * NB
+                part = h_grp[b, hf][:, lo:hi, :].rearrange("p (u n) t -> p u (n t)", n=16)
+                nc.vector.tensor_tensor(
+                    out=part, in0=part,
+                    in1=floor_bf[:, b:b + 1, :, :].rearrange("p u n t -> p u (n t)").to_broadcast([P, (hi - lo) // 16, 16 * PACK]),
+                    op=ALU.max)
+
+        def h_quantise(b, hf):
+            h_codes[b, hf] = sb("h_codes%d%d" % (b, hf), [P, HALF], U32)
+            h_scales[b, hf] = sb("h_scales%d%d" % (b, hf), [P, HALF], U8)
+            nc.vector.quantize_mx(out=h_codes[b, hf][:].bitcast(FP8X4), scales=h_scales[b, hf][:],
+                                  in_=h_grp[b, hf][:].rearrange("p n t -> p (n t)"))
+
+        wa_wd = sb("wa_wd", [P, 2, PACK, P], U16)
+        wa_sd = sb("wa_sd", [P, 2, PACK, P], U8)
+
+        def deal_wa():
+            nc.vector.tensor_copy(out=wa_wd[:], in_=wa_w[:].bitcast(U16).rearrange("p a (m t) -> p a t m", t=PACK))
+            nc.vector.tensor_copy(out=wa_sd[:], in_=wa_s[:].rearrange("p a (m t) -> p a t m", t=PACK))
+
+        e = [sb("e%d" % t, [P, S], F32) for t in range(PACK)]
+        look = sb("look", [P, PACK, M], F32)
+        sums = {}
+        held = {}
+
+        def ah_passes(t, hf):
+            sums["ah", t, hf] = psum.tile([P, HALF], F32, name="bank")
+            for b in range(2):
+                nc.tensor.matmul_mx(
+                    out=sums["ah", t, hf][:], lhsT=wa_wd[:, b, t, :].bitcast(U8).bitcast(FP4X4), lhsT_scale=wa_sd[:, b, t, :],
+                    rhs=h_codes[b, hf][:].bitcast(FP8X4), rhs_scale=h_scales[b, hf][:],
+                    start=(b == 0), stop=(b == 1),
+                )
+
+        def bv_passes(t, hf):
+            sums["bv", t, hf] = psum.tile([P, HALF], F32, name="bank")
+            for a in range(2):
+                name = "wb%d" % a
+                nc.tensor.matmul_mx(
+                    out=sums["bv", t, hf][:], lhsT=codes[name][:, t * P:(t + 1) * P].bitcast(FP8X4),
+                    lhsT_scale=scales[name][:, t * P:(t + 1) * P],
+                    rhs=v_w[a, hf][:].bitcast(FP8X4), rhs_scale=v_s[hf][4 * a:P, :],
+                    start=(a == 0), stop=(a == 1),
+                )
+
+        def hold(kind, t, hf):
+            held[t, hf] = sb("held%d%d" % (t, hf), [P, HALF], F32)
+            nc.scalar.copy(out=held[t, hf][:], in_=sums[kind, t, hf][:])
+
+        def score(kind, t, hf):
+            prod = ring.tile([P, HALF], F32, name="prod")
+            nc.vector.tensor_tensor(out=prod[:], in0=sums[kind, t, hf][:], in1=held[t, hf][:], op=ALU.mult)
+            nc.vector.tensor_scalar(out=e[t][:, hf * HALF:(hf + 1) * HALF], in0=prod[:], scalar1=2.0, scalar2=-2.0,
+                                    op0=ALU.min, op1=ALU.max)
+
+        def look_up(t):
+            nc.scalar.activation(out=look[:, t, :], in_=e[t][:].indirect(pos1_sb[:]), func=ACT.Exp,
+                                 bias=shift_sb[:, t:t + 1], scale=temp_sb[:, t:t + 1])
+
+        MH = M // 2
+        y_scales = sb("y_scales", [P, M], U8)
+        picked = [sb("picked%d" % mh, [P, PACK, MH], F32) for mh in range(2)]
+        diff = sb("diff", [P, PACK, M], F32)
+
+        def pick(t, mh):
+            nc.vector.tensor_copy(out=picked[mh][:, t, :], in_=e[t][:].indirect(pos2_sb[:, 16 * mh:16 * mh + 16]))
+
+        def subtract(t):
+            nc.vector.tensor_tensor(out=diff[:, t, :], in0=look[:, t, :], in1=base_sb[:, t, :], op=ALU.subtract)
+
+        def finish(mh, on_vector):
+            cols = slice(mh * MH, (mh + 1) * MH)
+            sine = sb("sine%d" % mh, [P, PACK, MH], F32)
+            nc.scalar.activation(out=sine[:], in_=picked[mh][:], func=ACT.Sin)
+            y = sb("y%d" % mh, [P, PACK, MH], F32)
+            nc.vector.tensor_tensor(out=y[:], in0=diff[:, :, cols], in1=sine[:], op=ALU.mult)
+            nc.sync.dma_start(out=out_0.rearrange("(p t) m -> p t m", t=PACK)[:, :, cols], in_=y[:])
+            y_grp = sb("y_grp%d" % mh, [P, MH, PACK], BF16)
+            dst = y_grp[:].rearrange("p (c i) t -> p c t i", i=4)
+            src = y[:].rearrange("p t (c i) -> p c t i", i=4)
+            if on_vector > 0:
+                nc.vector.tensor_copy(out=dst[:, 0:on_vector], in_=src[:, 0:on_vector])
+            if on_vector < MH // 4:
+                nc.scalar.copy(out=dst[:, on_vector:], in_=src[:, on_vector:])
+            y_codes = sb("y_codes%d" % mh, [P, MH], U32)
+            nc.vector.quantize_mx(out=y_codes[:].bitcast(FP8X4), scales=y_scales[:, cols],
+                                  in_=y_grp[:].rearrange("p m t -> p (m t)"))
+            nc.sync.dma_start(out=out_1[0].rearrange("p m t -> p (m t)").bitcast(I32)[:, cols], in_=y_codes[:].bitcast(I32))
+
+        gather_scales(0)
+        gather_scales(1)
+        cast_weight("w00", 0, 0)
+        gather_words(0, 0)
+        quantise_weight("w00")
+        gather_words(0, 1)
+        cast_weight("w01", 48, 0)
+        quantise_weight("w01")
+        gather_words(1, 0)
+        gather_words(1, 1)
+        cast_weight("w10", 0, 0)
+        quantise_weight("w10")
+        cast_weight("w11", 0, 0)
+        quantise_weight("w11")
+        h_passes(0, 0, 0)
+        h_passes(0, 0, 1)
+        h_passes(0, 1, 0)
+        h_passes(0, 1, 1)
+        h_exit(0, 0, "VVVV")
+        h_exit(0, 1, "VVVV")
+        h_passes(1, 0, 0)
+        h_passes(1, 0, 1)
+        h_passes(1, 1, 0)
+        h_passes(1, 1, 1)
+        h_quantise(0, 0)
+        h_exit(1, 0, "VVVV")
+        h_quantise(1, 0)
+        deal_wa()
+        h_quantise(0, 1)
+        h_exit(1, 1, "SSSS")
+        h_quantise(1, 1)
+        cast_weight("wb0", 0, 0)
+        quantise_weight("wb0")
+        cast_weight("wb1", 0, 0)
+        quantise_weight("wb1")
+        for t in range(PACK):
+            for hf in range(2):
+                ah_passes(t, hf)
+                bv_passes(t, hf)
+                hold("ah", t, hf)
+                score("bv", t, hf)
+            look_up(t)
+        for mh in range(2):
+            for t in range(PACK):
+                pick(t, mh)
+        for t in range(PACK):
+            subtract(t)
+        finish(0, 0)
+        finish(1, 48)
+        for q in range(4):
+            eng = nc.scalar if q % 2 else nc.sync
+            eng.dma_start(out=out_2[0, 4 * q:4 * q + 4, :].bitcast(I32), in_=y_scales[32 * q:32 * q + 4, :].bitcast(I32))

@@ -19,8 +19,38 @@ ACT = mybir.ActivationFunctionType
 P = 128
 PACK = 4
 KP = P * PACK
-HALF = 512
+HALF = S // 2
 NB = 128
+BANKS = HALF // NB
+MH = M // 2
+FLOOR_RUN = 16
+
+W00_ON_VECTOR = 32
+W01_ON_VECTOR = 80
+LAST_REGROUP_ON_VECTOR = 44
+
+BUFFER_OF = {
+    "v_w1": "grouped_w00",
+    "grouped_w01": "tab_w1",
+    "floor_bf": "tab_w1",
+    "wa_dealt_w": "raw_w01",
+    "grouped_w10": "wa_w",
+    "grouped_w11": "raw_w10",
+    "grouped_wb0": "raw_w11",
+    "grouped_wb1": "raw_wb0",
+    "codes_w10": "h_grp000",
+    "h_grp010": "wa_w",
+    "codes_w11": "h_grp001",
+    "wa_dealt_s": "raw_w10",
+    "codes_wb0": "wa_s",
+    "codes_wb1": "h_grp100",
+    "prod0": "h_grp110",
+    "prod1": "tab_w0",
+    "prod2": "tab_w1",
+    "prod3": "raw_wb1",
+    "picked": "raw_wb1",
+    "sine": "temp_sb",
+}
 
 
 def tile_list_burst_band_features_kernel(
@@ -30,11 +60,10 @@ def tile_list_burst_band_features_kernel(
     nc = tc.nc
     with ExitStack() as ctx:
         keep = ctx.enter_context(tc.tile_pool(name="keep", bufs=1))
-        ring = ctx.enter_context(tc.tile_pool(name="ring", bufs=3))
         psum = ctx.enter_context(tc.psum_pool(name="psum", bufs=8))
 
-        def sb(name, shape, dtype, tag=None):
-            return keep.tile(shape, dtype, name=name, tag=tag or name, align_bytes=64)
+        def sb(name, shape, dtype):
+            return keep.tile(shape, dtype, name=name, tag=BUFFER_OF.get(name, name), align_bytes=64)
 
         offs_sb = keep.tile([P, S // 16], U16, name="offs_sb")
         pos1_sb = keep.tile([P, M // 16], U16, name="pos1_sb")
@@ -51,259 +80,251 @@ def tile_list_burst_band_features_kernel(
         base_sb = sb("base_sb", [P, PACK, M], F32)
 
         nc.vector.memset(tab_s[:].bitcast(I32), 0)
-        nc.gpsimd.memset(wa_s[:].rearrange("p a n -> p (a n)").bitcast(I32), 0)
+        nc.gpsimd.memset(wa_s[:].rearrange("p b n -> p (b n)").bitcast(I32), 0)
 
-        raw = {}
         weight_rows = {"w%d%d" % (b, a): w1[a * KP:(a + 1) * KP, b * KP:(b + 1) * KP] for b in range(2) for a in range(2)}
         weight_rows.update({"wb%d" % a: wb[a * KP:(a + 1) * KP, :] for a in range(2)})
+        raw = {}
 
         def load_weight(name):
             raw[name] = sb("raw_" + name, [P, PACK, KP], F32)
             nc.sync.dma_start(out=raw[name][:], in_=weight_rows[name].rearrange("(p j) c -> p j c", j=PACK))
 
         def load_tab(a):
-            nc.sync.dma_start(out=tab_w[a][:].bitcast(I32), in_=tab_words[a].rearrange("p t i -> p (t i)").bitcast(I32))
-
-        def load_tab_scales():
-            for q in range(4):
-                nc.sync.dma_start(out=tab_s_rows[32 * q:32 * q + 8, :], in_=tab_scales[:, 4 * q:4 * q + 4, :].bitcast(I32))
-
-        def load_wa():
-            nc.sync.dma_start(out=wa_w[:].bitcast(I32), in_=wa_words.rearrange("a p c -> p a c").bitcast(I32))
-            for q in range(4):
-                nc.sync.dma_start(out=wa_s[32 * q:32 * q + 4, :, :].bitcast(I32),
-                                  in_=wa_scales[:, 4 * q:4 * q + 4, :].rearrange("a r n -> r a n").bitcast(I32))
-
-        def load_small(tile, vec):
-            nc.sync.dma_start(out=tile[:], in_=vec)
+            nc.sync.dma_start(out=tab_w[a][:].bitcast(I32), in_=tab_words[a].rearrange("p c j -> p (c j)").bitcast(I32))
 
         nc.sync.dma_start(offs_sb[:], offs)
-        load_small(floor_sb, floor.rearrange("(b p t) -> p b t", b=2, t=PACK))
-        load_tab_scales()
-        load_weight("w00")
+        for q in range(4):
+            nc.sync.dma_start(out=tab_s_rows[32 * q:32 * q + 8, :], in_=tab_scales[:, 4 * q:4 * q + 4, :].bitcast(I32))
         load_tab(0)
-        load_weight("w01")
+        load_weight("w00")
         load_tab(1)
+        load_weight("w01")
+        nc.sync.dma_start(out=floor_sb[:], in_=floor.rearrange("(b p t) -> p b t", b=2, t=PACK))
+        nc.sync.dma_start(out=wa_w[:].bitcast(I32), in_=wa_words.rearrange("b p c -> p b c").bitcast(I32))
         load_weight("w10")
         load_weight("w11")
-        load_wa()
+        for q in range(4):
+            nc.sync.dma_start(out=wa_s[32 * q:32 * q + 4, :, :].bitcast(I32),
+                              in_=wa_scales[:, 4 * q:4 * q + 4, :].rearrange("b r n -> r b n").bitcast(I32))
         load_weight("wb0")
         load_weight("wb1")
         nc.sync.dma_start(pos1_sb[:], pos1)
         nc.sync.dma_start(pos2_sb[:], pos2)
-        load_small(temp_sb, temp.rearrange("(p t) -> p t", t=PACK))
-        load_small(shift_sb, shift.rearrange("(p t) -> p t", t=PACK))
-        load_small(base_sb, base.rearrange("(p t) m -> p t m", t=PACK))
+        nc.sync.dma_start(out=temp_sb[:], in_=temp.rearrange("(p t) -> p t", t=PACK))
+        nc.sync.dma_start(out=shift_sb[:], in_=shift.rearrange("(p t) -> p t", t=PACK))
+        nc.sync.dma_start(out=base_sb[:], in_=base.rearrange("(p t) m -> p t m", t=PACK))
 
         for q in range(4):
             nc.vector.tensor_copy(out=tab_s[32 * q:32 * q + 8, :].bitcast(I32), in_=tab_s_rows[32 * q:32 * q + 8, :])
-        floor_bf = sb("floor_bf", [P, 2, 16, PACK], BF16)
-        nc.vector.tensor_copy(out=floor_bf[:], in_=floor_sb[:].unsqueeze(2).to_broadcast([P, 2, 16, PACK]))
 
-        codes = {}
-        scales = {}
-        grouped = {}
+        grouped, codes, scales = {}, {}, {}
 
-        def cast_weight(name, on_vector, on_gpsimd):
-            grouped[name] = ring.tile([P, PACK, P, PACK], BF16, name="grouped", align_bytes=64)
-            dst = grouped[name][:].rearrange("p t m j -> p m j t")
-            src = raw[name][:].rearrange("p j (m t) -> p m j t", t=PACK)
+        def prepare_weight(name, on_vector):
+            grouped[name] = sb("grouped_" + name, [P, PACK, P, PACK], BF16)
+            dst = grouped[name][:].rearrange("p t m (u v) -> p m u t v", v=2)
+            src = raw[name][:].rearrange("p (u v) (m t) -> p m u t v", v=2, t=PACK)
             if on_vector > 0:
                 nc.vector.tensor_copy(out=dst[:, 0:on_vector], in_=src[:, 0:on_vector])
-            for m0 in range(on_vector, on_vector + on_gpsimd, 32):
-                nc.gpsimd.tensor_scalar(out=dst[:, m0:m0 + 32], in0=src[:, m0:m0 + 32], scalar1=1.0, scalar2=0.0,
-                                        op0=ALU.mult, op1=ALU.add)
-            if on_vector + on_gpsimd < P:
-                nc.scalar.copy(out=dst[:, on_vector + on_gpsimd:P], in_=src[:, on_vector + on_gpsimd:P])
-
-        def quantise_weight(name):
+            nc.scalar.copy(out=dst[:, on_vector:P], in_=src[:, on_vector:P])
             codes[name] = sb("codes_" + name, [P, KP], U32)
             scales[name] = sb("scales_" + name, [P, KP], U8)
             nc.vector.quantize_mx(out=codes[name][:].bitcast(FP8X4), scales=scales[name][:],
                                   in_=grouped[name][:].rearrange("p t m j -> p (t m j)"))
 
         v_w = {}
-        v_s = {}
 
-        def gather_scales(hf):
-            v_s[hf] = sb("v_s%d" % hf, [P, HALF], U8)
-            nc.vector.tensor_copy(out=v_s[hf][:], in_=tab_s[:].indirect(offs_sb[:, 32 * hf:32 * hf + 32]))
+        def gather_words(a):
+            v_w[a] = sb("v_w%d" % a, [P, S], U32)
+            nc.vector.tensor_copy(out=v_w[a][:], in_=tab_w[a][:].indirect(offs_sb[:]))
 
-        def gather_words(a, hf):
-            v_w[a, hf] = sb("v_w%d%d" % (a, hf), [P, HALF], U32)
-            nc.vector.tensor_copy(out=v_w[a, hf][:], in_=tab_w[a][:].indirect(offs_sb[:, 32 * hf:32 * hf + 32]))
-
-        h_banks = {}
-        h_grp = {}
-        h_codes = {}
-        h_scales = {}
+        h_banks, h_grp, h_codes, h_scales = {}, {}, {}, {}
 
         def h_passes(b, a, hf):
             name = "w%d%d" % (b, a)
-            for i in range(HALF // NB):
+            for i in range(BANKS):
                 if a == 0:
                     h_banks[b, hf, i] = psum.tile([P, PACK, NB], F32, name="bank")
-                c0 = i * NB
+                cols = slice(hf * HALF + i * NB, hf * HALF + (i + 1) * NB)
                 for t in range(PACK):
                     nc.tensor.matmul_mx(
                         out=h_banks[b, hf, i][:, t, :],
                         lhsT=codes[name][:, t * P:(t + 1) * P].bitcast(FP8X4),
                         lhsT_scale=scales[name][:, t * P:(t + 1) * P],
-                        rhs=v_w[a, hf][:, c0:c0 + NB].bitcast(FP8X4),
-                        rhs_scale=v_s[hf][4 * a:P, c0:c0 + NB],
+                        rhs=v_w[a][:, cols].bitcast(FP8X4),
+                        rhs_scale=v_s[4 * a:P, cols],
                         start=(a == 0 and t == 0), stop=(a == 1 and t == PACK - 1),
                     )
 
-        def h_exit(b, hf, how):
-            h_grp[b, hf] = sb("h_grp%d%d" % (b, hf), [P, HALF, PACK], BF16)
-            on_scalar = []
-            for i in range(HALF // NB):
-                cols = h_grp[b, hf][:, i * NB:(i + 1) * NB, :]
-                sums = h_banks[b, hf, i][:].rearrange("p t n -> p n t")
-                if how[i] == "V":
-                    nc.vector.tensor_tensor(out=cols, in0=sums, in1=floor_sb[:, b:b + 1, :].to_broadcast([P, NB, PACK]), op=ALU.max)
-                else:
-                    nc.scalar.copy(out=cols, in_=sums)
-                    on_scalar.append(i)
-            if on_scalar:
-                lo, hi = on_scalar[0] * NB, (on_scalar[-1] + 1) * NB
-                part = h_grp[b, hf][:, lo:hi, :].rearrange("p (u n) t -> p u (n t)", n=16)
-                nc.vector.tensor_tensor(
-                    out=part, in0=part,
-                    in1=floor_bf[:, b:b + 1, :, :].rearrange("p u n t -> p u (n t)").to_broadcast([P, (hi - lo) // 16, 16 * PACK]),
-                    op=ALU.max)
+        def new_h_tiles(b, hf, parts):
+            h_grp[b, hf] = [sb("h_grp%d%d%d" % (b, hf, u), [P, HALF // parts, PACK], BF16) for u in range(parts)]
+
+        def h_views(b, hf, i):
+            per_part = BANKS // len(h_grp[b, hf])
+            first = (i % per_part) * NB
+            dst = h_grp[b, hf][i // per_part][:, first:first + NB, :].rearrange("p (c v) t -> p c t v", v=2)
+            return dst, h_banks[b, hf, i][:].rearrange("p t (c v) -> p c t v", v=2)
+
+        def h_exit_vector(b, hf, i):
+            dst, src = h_views(b, hf, i)
+            floors = floor_sb[:, b:b + 1, :].unsqueeze(3).to_broadcast([P, NB // 2, PACK, 2])
+            nc.vector.tensor_tensor(out=dst, in0=src, in1=floors, op=ALU.max)
 
         def h_quantise(b, hf):
             h_codes[b, hf] = sb("h_codes%d%d" % (b, hf), [P, HALF], U32)
             h_scales[b, hf] = sb("h_scales%d%d" % (b, hf), [P, HALF], U8)
-            nc.vector.quantize_mx(out=h_codes[b, hf][:].bitcast(FP8X4), scales=h_scales[b, hf][:],
-                                  in_=h_grp[b, hf][:].rearrange("p n t -> p (n t)"))
-
-        wa_wd = sb("wa_wd", [P, 2, PACK, P], U16)
-        wa_sd = sb("wa_sd", [P, 2, PACK, P], U8)
-
-        def deal_wa():
-            nc.vector.tensor_copy(out=wa_wd[:], in_=wa_w[:].bitcast(U16).rearrange("p a (m t) -> p a t m", t=PACK))
-            nc.vector.tensor_copy(out=wa_sd[:], in_=wa_s[:].rearrange("p a (m t) -> p a t m", t=PACK))
+            width = HALF // len(h_grp[b, hf])
+            for u, part in enumerate(h_grp[b, hf]):
+                nc.vector.quantize_mx(out=h_codes[b, hf][:, u * width:(u + 1) * width].bitcast(FP8X4),
+                                      scales=h_scales[b, hf][:, u * width:(u + 1) * width],
+                                      in_=part[:].rearrange("p c t -> p (c t)"))
 
         e = [sb("e%d" % t, [P, S], F32) for t in range(PACK)]
-        look = sb("look", [P, PACK, M], F32)
-        sums = {}
-        held = {}
+        held, prod = {}, {}
 
         def ah_passes(t, hf):
-            sums["ah", t, hf] = psum.tile([P, HALF], F32, name="bank")
+            bank = psum.tile([P, HALF], F32, name="bank")
             for b in range(2):
                 nc.tensor.matmul_mx(
-                    out=sums["ah", t, hf][:], lhsT=wa_wd[:, b, t, :].bitcast(U8).bitcast(FP4X4), lhsT_scale=wa_sd[:, b, t, :],
+                    out=bank[:], lhsT=wa_dealt_w[:, b, t, :].bitcast(U8).bitcast(FP4X4), lhsT_scale=wa_dealt_s[:, b, t, :],
                     rhs=h_codes[b, hf][:].bitcast(FP8X4), rhs_scale=h_scales[b, hf][:],
                     start=(b == 0), stop=(b == 1),
                 )
+            return bank
 
         def bv_passes(t, hf):
-            sums["bv", t, hf] = psum.tile([P, HALF], F32, name="bank")
+            bank = psum.tile([P, HALF], F32, name="bank")
             for a in range(2):
                 name = "wb%d" % a
                 nc.tensor.matmul_mx(
-                    out=sums["bv", t, hf][:], lhsT=codes[name][:, t * P:(t + 1) * P].bitcast(FP8X4),
+                    out=bank[:], lhsT=codes[name][:, t * P:(t + 1) * P].bitcast(FP8X4),
                     lhsT_scale=scales[name][:, t * P:(t + 1) * P],
-                    rhs=v_w[a, hf][:].bitcast(FP8X4), rhs_scale=v_s[hf][4 * a:P, :],
+                    rhs=v_w[a][:, hf * HALF:(hf + 1) * HALF].bitcast(FP8X4),
+                    rhs_scale=v_s[4 * a:P, hf * HALF:(hf + 1) * HALF],
                     start=(a == 0), stop=(a == 1),
                 )
+            return bank
 
-        def hold(kind, t, hf):
+        def hold(bank, t, hf):
             held[t, hf] = sb("held%d%d" % (t, hf), [P, HALF], F32)
-            nc.scalar.copy(out=held[t, hf][:], in_=sums[kind, t, hf][:])
+            nc.scalar.copy(out=held[t, hf][:], in_=bank[:])
 
-        def score(kind, t, hf):
-            prod = ring.tile([P, HALF], F32, name="prod")
-            nc.vector.tensor_tensor(out=prod[:], in0=sums[kind, t, hf][:], in1=held[t, hf][:], op=ALU.mult)
-            nc.vector.tensor_scalar(out=e[t][:, hf * HALF:(hf + 1) * HALF], in0=prod[:], scalar1=2.0, scalar2=-2.0,
-                                    op0=ALU.min, op1=ALU.max)
+        def score(bank, t, hf, limit_engine):
+            if hf == 0:
+                prod[t] = sb("prod%d" % t, [P, S], F32)
+            cols = slice(hf * HALF, (hf + 1) * HALF)
+            nc.vector.tensor_tensor(out=prod[t][:, cols], in0=bank[:], in1=held[t, hf][:], op=ALU.mult)
+            limit_engine.tensor_scalar(out=e[t][:, cols], in0=prod[t][:, cols], scalar1=2.0, scalar2=-2.0,
+                                       op0=ALU.min, op1=ALU.max)
 
-        def look_up(t):
+        y_scales = sb("y_scales", [P, M], U8)
+
+        v_s = sb("v_s", [P, S], U8)
+        nc.vector.tensor_copy(out=v_s[:], in_=tab_s[:].indirect(offs_sb[:]))
+        gather_words(0)
+        prepare_weight("w00", W00_ON_VECTOR)
+        gather_words(1)
+        prepare_weight("w01", W01_ON_VECTOR)
+
+        wa_dealt_w = sb("wa_dealt_w", [P, 2, PACK, P], U16)
+        nc.scalar.copy(out=wa_dealt_w[:].rearrange("p b t (u v) -> p b u t v", v=2),
+                       in_=wa_w[:].bitcast(U16).rearrange("p b (u v t) -> p b u t v", v=2, t=PACK))
+
+        for a in range(2):
+            for hf in range(2):
+                h_passes(0, a, hf)
+        new_h_tiles(0, 0, 2)
+        for i in range(BANKS):
+            h_exit_vector(0, 0, i)
+        h_quantise(0, 0)
+        prepare_weight("w10", 0)
+        new_h_tiles(0, 1, 1)
+        for i in range(BANKS):
+            h_exit_vector(0, 1, i)
+        prepare_weight("w11", 0)
+        h_quantise(0, 1)
+
+        wa_dealt_s = sb("wa_dealt_s", [P, 2, PACK, P], U8)
+        nc.vector.tensor_copy(out=wa_dealt_s[:].rearrange("p b t (u v) -> p b u t v", v=4),
+                              in_=wa_s[:].rearrange("p b (u v t) -> p b u t v", v=4, t=PACK))
+
+        for a in range(2):
+            for hf in range(2):
+                h_passes(1, a, hf)
+        floor_bf = sb("floor_bf", [P, FLOOR_RUN, PACK], BF16)
+        nc.vector.tensor_copy(out=floor_bf[:], in_=floor_sb[:, 1:2, :].to_broadcast([P, FLOOR_RUN, PACK]))
+        new_h_tiles(1, 0, 1)
+        for i in range(BANKS):
+            h_exit_vector(1, 0, i)
+        prepare_weight("wb0", 0)
+        h_quantise(1, 0)
+        new_h_tiles(1, 1, 1)
+        h_exit_vector(1, 1, 0)
+        prepare_weight("wb1", 0)
+        h_exit_vector(1, 1, 1)
+        for i in range(2, BANKS):
+            dst, src = h_views(1, 1, i)
+            nc.scalar.copy(out=dst, in_=src)
+        unfloored = h_grp[1, 1][0][:, 2 * NB:, :].rearrange("p (u c) t -> p u (c t)", c=FLOOR_RUN)
+        runs = floor_bf[:].rearrange("p c t -> p (c t)").unsqueeze(1).to_broadcast([P, 2 * NB // FLOOR_RUN, FLOOR_RUN * PACK])
+        nc.vector.tensor_tensor(out=unfloored, in0=unfloored, in1=runs, op=ALU.max)
+        h_quantise(1, 1)
+
+        for t in range(PACK):
+            hold(ah_passes(t, 0), t, 0)
+        for t in range(PACK):
+            score(bv_passes(t, 0), t, 0, nc.gpsimd)
+        hold(bv_passes(0, 1), 0, 1)
+        for t in range(PACK):
+            if t + 1 < PACK:
+                hold(bv_passes(t + 1, 1), t + 1, 1)
+            score(ah_passes(t, 1), t, 1, nc.gpsimd if t == 0 else nc.vector)
+
+        look = sb("look", [P, PACK, M], F32)
+        for t in range(PACK):
             nc.scalar.activation(out=look[:, t, :], in_=e[t][:].indirect(pos1_sb[:]), func=ACT.Exp,
                                  bias=shift_sb[:, t:t + 1], scale=temp_sb[:, t:t + 1])
+        picked = sb("picked", [P, PACK, M], F32)
+        for t in range(PACK):
+            nc.vector.tensor_copy(out=picked[:, t, :], in_=e[t][:].indirect(pos2_sb[:]))
 
-        MH = M // 2
-        y_scales = sb("y_scales", [P, M], U8)
-        picked = [sb("picked%d" % mh, [P, PACK, MH], F32) for mh in range(2)]
-        diff = sb("diff", [P, PACK, M], F32)
+        sine = sb("sine", [P, PACK, M], F32)
+        for rows, cols in ((slice(0, 2), slice(0, MH)), (slice(2, PACK), slice(0, MH)), (slice(0, PACK), slice(MH, M))):
+            nc.scalar.activation(out=sine[:, rows, cols], in_=picked[:, rows, cols], func=ACT.Sin)
 
-        def pick(t, mh):
-            nc.vector.tensor_copy(out=picked[mh][:, t, :], in_=e[t][:].indirect(pos2_sb[:, 16 * mh:16 * mh + 16]))
+        out_rows = out_0.rearrange("(p t) m -> p t m", t=PACK)
+        out_words = out_1[0].rearrange("p m t -> p (m t)").bitcast(I32)
+        y, y_grp = {}, {}
 
-        def subtract(t):
-            nc.vector.tensor_tensor(out=diff[:, t, :], in0=look[:, t, :], in1=base_sb[:, t, :], op=ALU.subtract)
-
-        def finish(mh, on_vector):
+        def features(mh):
             cols = slice(mh * MH, (mh + 1) * MH)
-            sine = sb("sine%d" % mh, [P, PACK, MH], F32)
-            nc.scalar.activation(out=sine[:], in_=picked[mh][:], func=ACT.Sin)
-            y = sb("y%d" % mh, [P, PACK, MH], F32)
-            nc.vector.tensor_tensor(out=y[:], in0=diff[:, :, cols], in1=sine[:], op=ALU.mult)
-            nc.sync.dma_start(out=out_0.rearrange("(p t) m -> p t m", t=PACK)[:, :, cols], in_=y[:])
-            y_grp = sb("y_grp%d" % mh, [P, MH, PACK], BF16)
-            dst = y_grp[:].rearrange("p (c i) t -> p c t i", i=4)
-            src = y[:].rearrange("p t (c i) -> p c t i", i=4)
+            diff = sb("diff%d" % mh, [P, PACK, MH], F32)
+            nc.vector.tensor_tensor(out=diff[:], in0=look[:, :, cols], in1=base_sb[:, :, cols], op=ALU.subtract)
+            y[mh] = sb("y%d" % mh, [P, PACK, MH], F32)
+            nc.vector.tensor_tensor(out=y[mh][:], in0=diff[:], in1=sine[:, :, cols], op=ALU.mult)
+            nc.sync.dma_start(out=out_rows[:, :, cols], in_=y[mh][:])
+
+        def regroup(mh, on_vector):
+            y_grp[mh] = sb("y_grp%d" % mh, [P, MH, PACK], BF16)
+            dst = y_grp[mh][:].rearrange("p (c v) t -> p c t v", v=4)
+            src = y[mh][:].rearrange("p t (c v) -> p c t v", v=4)
             if on_vector > 0:
                 nc.vector.tensor_copy(out=dst[:, 0:on_vector], in_=src[:, 0:on_vector])
-            if on_vector < MH // 4:
-                nc.scalar.copy(out=dst[:, on_vector:], in_=src[:, on_vector:])
+            nc.scalar.copy(out=dst[:, on_vector:], in_=src[:, on_vector:])
+
+        def emit_planes(mh):
+            cols = slice(mh * MH, (mh + 1) * MH)
             y_codes = sb("y_codes%d" % mh, [P, MH], U32)
             nc.vector.quantize_mx(out=y_codes[:].bitcast(FP8X4), scales=y_scales[:, cols],
-                                  in_=y_grp[:].rearrange("p m t -> p (m t)"))
-            nc.sync.dma_start(out=out_1[0].rearrange("p m t -> p (m t)").bitcast(I32)[:, cols], in_=y_codes[:].bitcast(I32))
+                                  in_=y_grp[mh][:].rearrange("p m t -> p (m t)"))
+            nc.sync.dma_start(out=out_words[:, cols], in_=y_codes[:].bitcast(I32))
 
-        gather_scales(0)
-        gather_scales(1)
-        cast_weight("w00", 0, 0)
-        gather_words(0, 0)
-        quantise_weight("w00")
-        gather_words(0, 1)
-        cast_weight("w01", 48, 0)
-        quantise_weight("w01")
-        gather_words(1, 0)
-        gather_words(1, 1)
-        cast_weight("w10", 0, 0)
-        quantise_weight("w10")
-        cast_weight("w11", 0, 0)
-        quantise_weight("w11")
-        h_passes(0, 0, 0)
-        h_passes(0, 0, 1)
-        h_passes(0, 1, 0)
-        h_passes(0, 1, 1)
-        h_exit(0, 0, "VVVV")
-        h_exit(0, 1, "VVVV")
-        h_passes(1, 0, 0)
-        h_passes(1, 0, 1)
-        h_passes(1, 1, 0)
-        h_passes(1, 1, 1)
-        h_quantise(0, 0)
-        h_exit(1, 0, "VVVV")
-        h_quantise(1, 0)
-        deal_wa()
-        h_quantise(0, 1)
-        h_exit(1, 1, "SSSS")
-        h_quantise(1, 1)
-        cast_weight("wb0", 0, 0)
-        quantise_weight("wb0")
-        cast_weight("wb1", 0, 0)
-        quantise_weight("wb1")
-        for t in range(PACK):
-            for hf in range(2):
-                ah_passes(t, hf)
-                bv_passes(t, hf)
-                hold("ah", t, hf)
-                score("bv", t, hf)
-            look_up(t)
-        for mh in range(2):
-            for t in range(PACK):
-                pick(t, mh)
-        for t in range(PACK):
-            subtract(t)
-        finish(0, 0)
-        finish(1, 48)
+        features(0)
+        regroup(0, 0)
+        features(1)
+        emit_planes(0)
+        regroup(1, LAST_REGROUP_ON_VECTOR)
+        emit_planes(1)
         for q in range(4):
-            eng = nc.scalar if q % 2 else nc.sync
-            eng.dma_start(out=out_2[0, 4 * q:4 * q + 4, :].bitcast(I32), in_=y_scales[32 * q:32 * q + 4, :].bitcast(I32))
+            queue = nc.scalar if q % 2 else nc.sync
+            queue.dma_start(out=out_2[0, 4 * q:4 * q + 4, :].bitcast(I32), in_=y_scales[32 * q:32 * q + 4, :].bitcast(I32))

from contextlib import ExitStack

import concourse.mybir as mybir

K, H, N, T, S, M = 1024, 1024, 512, 2048, 1024, 512
FLOPS = 2 * S * (K * H + H * N + K * N)

F32 = mybir.dt.float32
BF16 = mybir.dt.bfloat16
I32 = mybir.dt.int32
U32 = mybir.dt.uint32
U16 = mybir.dt.uint16
U8 = mybir.dt.uint8
FP8X4 = mybir.dt.float8_e4m3fn_x4
FP4X4 = mybir.dt.float4_e2m1fn_x4
ALU = mybir.AluOpType
ACT = mybir.ActivationFunctionType

P = 128
PACK = 4
KP = P * PACK
HALF = S // 2
NB = 128
BANKS = HALF // NB
MH = M // 2
FLOOR_RUN = 16

W00_ON_VECTOR = 32
W01_ON_VECTOR = 80
LAST_REGROUP_ON_VECTOR = 44

BUFFER_OF = {
    "v_w1": "grouped_w00",
    "grouped_w01": "tab_w1",
    "floor_bf": "tab_w1",
    "wa_dealt_w": "raw_w01",
    "grouped_w10": "wa_w",
    "grouped_w11": "raw_w10",
    "grouped_wb0": "raw_w11",
    "grouped_wb1": "raw_wb0",
    "codes_w10": "h_grp000",
    "h_grp010": "wa_w",
    "codes_w11": "h_grp001",
    "wa_dealt_s": "raw_w10",
    "codes_wb0": "wa_s",
    "codes_wb1": "h_grp100",
    "prod0": "h_grp110",
    "prod1": "tab_w0",
    "prod2": "tab_w1",
    "prod3": "raw_wb1",
    "picked": "raw_wb1",
    "sine": "temp_sb",
}


def tile_list_burst_band_features_kernel(
    tc, tab_words, tab_scales, offs, pos1, pos2, w1, floor, wa_words, wa_scales, wb, temp, shift, base,
    out_0, out_1, out_2,
):
    nc = tc.nc
    with ExitStack() as ctx:
        keep = ctx.enter_context(tc.tile_pool(name="keep", bufs=1))
        psum = ctx.enter_context(tc.psum_pool(name="psum", bufs=8))

        def sb(name, shape, dtype):
            return keep.tile(shape, dtype, name=name, tag=BUFFER_OF.get(name, name), align_bytes=64)

        offs_sb = keep.tile([P, S // 16], U16, name="offs_sb")
        pos1_sb = keep.tile([P, M // 16], U16, name="pos1_sb")
        pos2_sb = keep.tile([P, M // 16], U16, name="pos2_sb")

        tab_w = [sb("tab_w%d" % a, [P, T], U32) for a in range(2)]
        tab_s = sb("tab_s", [P, T], U8)
        tab_s_rows = sb("tab_s_rows", [P, T // 4], I32)
        wa_w = sb("wa_w", [P, 2, 2 * N], U8)
        wa_s = sb("wa_s", [P, 2, N], U8)
        floor_sb = sb("floor_sb", [P, 2, PACK], F32)
        temp_sb = sb("temp_sb", [P, PACK], F32)
        shift_sb = sb("shift_sb", [P, PACK], F32)
        base_sb = sb("base_sb", [P, PACK, M], F32)

        nc.vector.memset(tab_s[:].bitcast(I32), 0)
        nc.gpsimd.memset(wa_s[:].rearrange("p b n -> p (b n)").bitcast(I32), 0)

        weight_rows = {"w%d%d" % (b, a): w1[a * KP:(a + 1) * KP, b * KP:(b + 1) * KP] for b in range(2) for a in range(2)}
        weight_rows.update({"wb%d" % a: wb[a * KP:(a + 1) * KP, :] for a in range(2)})
        raw = {}

        def load_weight(name):
            raw[name] = sb("raw_" + name, [P, PACK, KP], F32)
            nc.sync.dma_start(out=raw[name][:], in_=weight_rows[name].rearrange("(p j) c -> p j c", j=PACK))

        def load_tab(a):
            nc.sync.dma_start(out=tab_w[a][:].bitcast(I32), in_=tab_words[a].rearrange("p c j -> p (c j)").bitcast(I32))

        nc.sync.dma_start(offs_sb[:], offs)
        for q in range(4):
            nc.sync.dma_start(out=tab_s_rows[32 * q:32 * q + 8, :], in_=tab_scales[:, 4 * q:4 * q + 4, :].bitcast(I32))
        load_tab(0)
        load_weight("w00")
        load_tab(1)
        load_weight("w01")
        nc.sync.dma_start(out=floor_sb[:], in_=floor.rearrange("(b p t) -> p b t", b=2, t=PACK))
        nc.sync.dma_start(out=wa_w[:].bitcast(I32), in_=wa_words.rearrange("b p c -> p b c").bitcast(I32))
        load_weight("w10")
        load_weight("w11")
        for q in range(4):
            nc.sync.dma_start(out=wa_s[32 * q:32 * q + 4, :, :].bitcast(I32),
                              in_=wa_scales[:, 4 * q:4 * q + 4, :].rearrange("b r n -> r b n").bitcast(I32))
        load_weight("wb0")
        load_weight("wb1")
        nc.sync.dma_start(pos1_sb[:], pos1)
        nc.sync.dma_start(pos2_sb[:], pos2)
        nc.sync.dma_start(out=temp_sb[:], in_=temp.rearrange("(p t) -> p t", t=PACK))
        nc.sync.dma_start(out=shift_sb[:], in_=shift.rearrange("(p t) -> p t", t=PACK))
        nc.sync.dma_start(out=base_sb[:], in_=base.rearrange("(p t) m -> p t m", t=PACK))

        for q in range(4):
            nc.vector.tensor_copy(out=tab_s[32 * q:32 * q + 8, :].bitcast(I32), in_=tab_s_rows[32 * q:32 * q + 8, :])

        grouped, codes, scales = {}, {}, {}

        def prepare_weight(name, on_vector):
            grouped[name] = sb("grouped_" + name, [P, PACK, P, PACK], BF16)
            dst = grouped[name][:].rearrange("p t m (u v) -> p m u t v", v=2)
            src = raw[name][:].rearrange("p (u v) (m t) -> p m u t v", v=2, t=PACK)
            if on_vector > 0:
                nc.vector.tensor_copy(out=dst[:, 0:on_vector], in_=src[:, 0:on_vector])
            nc.scalar.copy(out=dst[:, on_vector:P], in_=src[:, on_vector:P])
            codes[name] = sb("codes_" + name, [P, KP], U32)
            scales[name] = sb("scales_" + name, [P, KP], U8)
            nc.vector.quantize_mx(out=codes[name][:].bitcast(FP8X4), scales=scales[name][:],
                                  in_=grouped[name][:].rearrange("p t m j -> p (t m j)"))

        v_w = {}

        def gather_words(a):
            v_w[a] = sb("v_w%d" % a, [P, S], U32)
            nc.vector.tensor_copy(out=v_w[a][:], in_=tab_w[a][:].indirect(offs_sb[:]))

        h_banks, h_grp, h_codes, h_scales = {}, {}, {}, {}

        def h_passes(b, a, hf):
            name = "w%d%d" % (b, a)
            for i in range(BANKS):
                if a == 0:
                    h_banks[b, hf, i] = psum.tile([P, PACK, NB], F32, name="bank")
                cols = slice(hf * HALF + i * NB, hf * HALF + (i + 1) * NB)
                for t in range(PACK):
                    nc.tensor.matmul_mx(
                        out=h_banks[b, hf, i][:, t, :],
                        lhsT=codes[name][:, t * P:(t + 1) * P].bitcast(FP8X4),
                        lhsT_scale=scales[name][:, t * P:(t + 1) * P],
                        rhs=v_w[a][:, cols].bitcast(FP8X4),
                        rhs_scale=v_s[4 * a:P, cols],
                        start=(a == 0 and t == 0), stop=(a == 1 and t == PACK - 1),
                    )

        def new_h_tiles(b, hf, parts):
            h_grp[b, hf] = [sb("h_grp%d%d%d" % (b, hf, u), [P, HALF // parts, PACK], BF16) for u in range(parts)]

        def h_views(b, hf, i):
            per_part = BANKS // len(h_grp[b, hf])
            first = (i % per_part) * NB
            dst = h_grp[b, hf][i // per_part][:, first:first + NB, :].rearrange("p (c v) t -> p c t v", v=2)
            return dst, h_banks[b, hf, i][:].rearrange("p t (c v) -> p c t v", v=2)

        def h_exit_vector(b, hf, i):
            dst, src = h_views(b, hf, i)
            floors = floor_sb[:, b:b + 1, :].unsqueeze(3).to_broadcast([P, NB // 2, PACK, 2])
            nc.vector.tensor_tensor(out=dst, in0=src, in1=floors, op=ALU.max)

        def h_quantise(b, hf):
            h_codes[b, hf] = sb("h_codes%d%d" % (b, hf), [P, HALF], U32)
            h_scales[b, hf] = sb("h_scales%d%d" % (b, hf), [P, HALF], U8)
            width = HALF // len(h_grp[b, hf])
            for u, part in enumerate(h_grp[b, hf]):
                nc.vector.quantize_mx(out=h_codes[b, hf][:, u * width:(u + 1) * width].bitcast(FP8X4),
                                      scales=h_scales[b, hf][:, u * width:(u + 1) * width],
                                      in_=part[:].rearrange("p c t -> p (c t)"))

        e = [sb("e%d" % t, [P, S], F32) for t in range(PACK)]
        held, prod = {}, {}

        def ah_passes(t, hf):
            bank = psum.tile([P, HALF], F32, name="bank")
            for b in range(2):
                nc.tensor.matmul_mx(
                    out=bank[:], lhsT=wa_dealt_w[:, b, t, :].bitcast(U8).bitcast(FP4X4), lhsT_scale=wa_dealt_s[:, b, t, :],
                    rhs=h_codes[b, hf][:].bitcast(FP8X4), rhs_scale=h_scales[b, hf][:],
                    start=(b == 0), stop=(b == 1),
                )
            return bank

        def bv_passes(t, hf):
            bank = psum.tile([P, HALF], F32, name="bank")
            for a in range(2):
                name = "wb%d" % a
                nc.tensor.matmul_mx(
                    out=bank[:], lhsT=codes[name][:, t * P:(t + 1) * P].bitcast(FP8X4),
                    lhsT_scale=scales[name][:, t * P:(t + 1) * P],
                    rhs=v_w[a][:, hf * HALF:(hf + 1) * HALF].bitcast(FP8X4),
                    rhs_scale=v_s[4 * a:P, hf * HALF:(hf + 1) * HALF],
                    start=(a == 0), stop=(a == 1),
                )
            return bank

        def hold(bank, t, hf):
            held[t, hf] = sb("held%d%d" % (t, hf), [P, HALF], F32)
            nc.scalar.copy(out=held[t, hf][:], in_=bank[:])

        def score(bank, t, hf, limit_engine):
            if hf == 0:
                prod[t] = sb("prod%d" % t, [P, S], F32)
            cols = slice(hf * HALF, (hf + 1) * HALF)
            nc.vector.tensor_tensor(out=prod[t][:, cols], in0=bank[:], in1=held[t, hf][:], op=ALU.mult)
            limit_engine.tensor_scalar(out=e[t][:, cols], in0=prod[t][:, cols], scalar1=2.0, scalar2=-2.0,
                                       op0=ALU.min, op1=ALU.max)

        y_scales = sb("y_scales", [P, M], U8)

        v_s = sb("v_s", [P, S], U8)
        nc.vector.tensor_copy(out=v_s[:], in_=tab_s[:].indirect(offs_sb[:]))
        gather_words(0)
        prepare_weight("w00", W00_ON_VECTOR)
        gather_words(1)
        prepare_weight("w01", W01_ON_VECTOR)

        wa_dealt_w = sb("wa_dealt_w", [P, 2, PACK, P], U16)
        nc.scalar.copy(out=wa_dealt_w[:].rearrange("p b t (u v) -> p b u t v", v=2),
                       in_=wa_w[:].bitcast(U16).rearrange("p b (u v t) -> p b u t v", v=2, t=PACK))

        for a in range(2):
            for hf in range(2):
                h_passes(0, a, hf)
        new_h_tiles(0, 0, 2)
        for i in range(BANKS):
            h_exit_vector(0, 0, i)
        h_quantise(0, 0)
        prepare_weight("w10", 0)
        new_h_tiles(0, 1, 1)
        for i in range(BANKS):
            h_exit_vector(0, 1, i)
        prepare_weight("w11", 0)
        h_quantise(0, 1)

        wa_dealt_s = sb("wa_dealt_s", [P, 2, PACK, P], U8)
        nc.vector.tensor_copy(out=wa_dealt_s[:].rearrange("p b t (u v) -> p b u t v", v=4),
                              in_=wa_s[:].rearrange("p b (u v t) -> p b u t v", v=4, t=PACK))

        for a in range(2):
            for hf in range(2):
                h_passes(1, a, hf)
        floor_bf = sb("floor_bf", [P, FLOOR_RUN, PACK], BF16)
        nc.vector.tensor_copy(out=floor_bf[:], in_=floor_sb[:, 1:2, :].to_broadcast([P, FLOOR_RUN, PACK]))
        new_h_tiles(1, 0, 1)
        for i in range(BANKS):
            h_exit_vector(1, 0, i)
        prepare_weight("wb0", 0)
        h_quantise(1, 0)
        new_h_tiles(1, 1, 1)
        h_exit_vector(1, 1, 0)
        prepare_weight("wb1", 0)
        h_exit_vector(1, 1, 1)
        for i in range(2, BANKS):
            dst, src = h_views(1, 1, i)
            nc.scalar.copy(out=dst, in_=src)
        unfloored = h_grp[1, 1][0][:, 2 * NB:, :].rearrange("p (u c) t -> p u (c t)", c=FLOOR_RUN)
        runs = floor_bf[:].rearrange("p c t -> p (c t)").unsqueeze(1).to_broadcast([P, 2 * NB // FLOOR_RUN, FLOOR_RUN * PACK])
        nc.vector.tensor_tensor(out=unfloored, in0=unfloored, in1=runs, op=ALU.max)
        h_quantise(1, 1)

        for t in range(PACK):
            hold(ah_passes(t, 0), t, 0)
        for t in range(PACK):
            score(bv_passes(t, 0), t, 0, nc.gpsimd)
        hold(bv_passes(0, 1), 0, 1)
        for t in range(PACK):
            if t + 1 < PACK:
                hold(bv_passes(t + 1, 1), t + 1, 1)
            score(ah_passes(t, 1), t, 1, nc.gpsimd if t == 0 else nc.vector)

        look = sb("look", [P, PACK, M], F32)
        for t in range(PACK):
            nc.scalar.activation(out=look[:, t, :], in_=e[t][:].indirect(pos1_sb[:]), func=ACT.Exp,
                                 bias=shift_sb[:, t:t + 1], scale=temp_sb[:, t:t + 1])
        picked = sb("picked", [P, PACK, M], F32)
        for t in range(PACK):
            nc.vector.tensor_copy(out=picked[:, t, :], in_=e[t][:].indirect(pos2_sb[:]))

        sine = sb("sine", [P, PACK, M], F32)
        for rows, cols in ((slice(0, 2), slice(0, MH)), (slice(2, PACK), slice(0, MH)), (slice(0, PACK), slice(MH, M))):
            nc.scalar.activation(out=sine[:, rows, cols], in_=picked[:, rows, cols], func=ACT.Sin)

        out_rows = out_0.rearrange("(p t) m -> p t m", t=PACK)
        out_words = out_1[0].rearrange("p m t -> p (m t)").bitcast(I32)
        y, y_grp = {}, {}

        def features(mh):
            cols = slice(mh * MH, (mh + 1) * MH)
            diff = sb("diff%d" % mh, [P, PACK, MH], F32)
            nc.vector.tensor_tensor(out=diff[:], in0=look[:, :, cols], in1=base_sb[:, :, cols], op=ALU.subtract)
            y[mh] = sb("y%d" % mh, [P, PACK, MH], F32)
            nc.vector.tensor_tensor(out=y[mh][:], in0=diff[:], in1=sine[:, :, cols], op=ALU.mult)
            nc.sync.dma_start(out=out_rows[:, :, cols], in_=y[mh][:])

        def regroup(mh, on_vector):
            y_grp[mh] = sb("y_grp%d" % mh, [P, MH, PACK], BF16)
            dst = y_grp[mh][:].rearrange("p (c v) t -> p c t v", v=4)
            src = y[mh][:].rearrange("p t (c v) -> p c t v", v=4)
            if on_vector > 0:
                nc.vector.tensor_copy(out=dst[:, 0:on_vector], in_=src[:, 0:on_vector])
            nc.scalar.copy(out=dst[:, on_vector:], in_=src[:, on_vector:])

        def emit_planes(mh):
            cols = slice(mh * MH, (mh + 1) * MH)
            y_codes = sb("y_codes%d" % mh, [P, MH], U32)
            nc.vector.quantize_mx(out=y_codes[:].bitcast(FP8X4), scales=y_scales[:, cols],
                                  in_=y_grp[mh][:].rearrange("p m t -> p (m t)"))
            nc.sync.dma_start(out=out_words[:, cols], in_=y_codes[:].bitcast(I32))

        features(0)
        regroup(0, 0)
        features(1)
        emit_planes(0)
        regroup(1, LAST_REGROUP_ON_VECTOR)
        emit_planes(1)
        for q in range(4):
            queue = nc.scalar if q % 2 else nc.sync
            queue.dma_start(out=out_2[0, 4 * q:4 * q + 4, :].bitcast(I32), in_=y_scales[32 * q:32 * q + 4, :].bitcast(I32))
